import numpy as np
import ml_dtypes


def mxq(x, axis, fmt="e4m3"):
    dtype, down = {"e4m3": (ml_dtypes.float8_e4m3fn, 7), "e5m2": (ml_dtypes.float8_e5m2, 14)}[fmt]
    v = np.moveaxis(np.asarray(x, np.float32).astype(ml_dtypes.bfloat16).astype(np.float64), axis, -1)
    blocks = v.reshape(v.shape[:-1] + (-1, 32))
    amax = np.abs(blocks).max(-1, keepdims=True)
    byte = np.maximum(np.where(amax > 0, np.frexp(amax)[1] - 1 + 127, 0) - down, 1)
    scale = np.exp2(byte - 127.0)
    codes = (blocks / scale).astype(np.float32).astype(dtype).astype(np.float64)
    return np.moveaxis((codes * scale).reshape(v.shape), -1, axis)


WIDE = False


def mx_kscale(k):
    if not WIDE:
        return np.ones(k)
    levels = np.array([30, -30])
    if k % 512:
        return np.exp2(np.random.permutation(np.resize(levels, k // 32))).repeat(32)
    a = np.empty((k // 512, 16))
    for p in range(k // 512):
        a[p, :8] = np.random.permutation(np.resize(levels, 8))
        for g in range(8):
            far = levels[np.abs(levels - a[p, g]) >= 10]
            a[p, g + 8] = far[np.random.randint(len(far))]
    return np.exp2(a.ravel()).repeat(32)


def f64(x):
    return np.asarray(x).astype(np.float64)


def striped(idx):
    return np.tile(np.asarray(idx).reshape(-1, 16).T, (8, 1)).astype(np.uint16)


def unstriped(offs):
    return offs[:16].T.reshape(-1).astype(np.int64)


E2M1 = np.array([0.0, 0.5, 1.0, 1.5, 2.0, 3.0, 4.0, 6.0, -0.0, -0.5, -1.0, -1.5, -2.0, -3.0, -4.0, -6.0])


def pack_weight(w, fmt):
    k, n = w.shape
    w = f64(np.asarray(w, np.float32).astype(ml_dtypes.bfloat16)).reshape(k // 32, 32, n)
    amax = np.abs(w).max(1)
    if fmt in ("e4m3", "e5m2"):
        byte = np.frexp(amax)[1] - 1 + 127 - (7 if fmt == "e4m3" else 14)
    else:
        mant, ex = np.frexp(amax / 6.0)
        byte = np.where(mant > 0.5, ex, ex - 1) + 127
    byte = np.clip(np.where(amax > 0, byte, 1), 1, 254)
    scaled = (w * np.exp2(127.0 - byte)[:, None, :]).reshape(k, n).astype(np.float32)
    by_word = np.ascontiguousarray(scaled.reshape(k // 512, 128, 4, n).transpose(0, 1, 3, 2))
    if fmt in ("e4m3", "e5m2"):
        words = by_word.astype(ml_dtypes.float8_e4m3fn if fmt == "e4m3" else ml_dtypes.float8_e5m2).view(np.uint8)
    else:
        c = by_word.astype(ml_dtypes.float4_e2m1fn).view(np.uint8) & 0xF
        words = (c[..., 0::2] | (c[..., 1::2] << 4)).reshape(k // 512, 128, 2 * n)
    return np.ascontiguousarray(words), np.ascontiguousarray(byte.astype(np.uint8).reshape(k // 512, 16, n))


def unpack_weight(words, scales, fmt):
    g, _, n = scales.shape
    words = np.ascontiguousarray(words).reshape(g, 128, n, -1)
    if fmt in ("e4m3", "e5m2"):
        vals = words.view(ml_dtypes.float8_e4m3fn if fmt == "e4m3" else ml_dtypes.float8_e5m2).astype(np.float64)
    else:
        nib = np.empty((g, 128, n, 4), np.uint8)
        nib[..., 0::2] = words & 0xF
        nib[..., 1::2] = words >> 4
        vals = E2M1[nib]
    vals = vals * np.repeat(np.exp2(scales.astype(np.float64) - 127.0), 8, axis=1)[..., None]
    return vals.transpose(0, 1, 3, 2).reshape(g * 512, n)


def sgn(shape):
    return np.random.uniform(0.5, 2.0, shape) * np.where(np.random.standard_normal(shape) < 0, -1.0, 1.0)


K, T, J, R, C, D, O, N = 512, 2048, 256, 512, 512, 512, 256, 256


def setup_inputs():
    n = np.random.standard_normal
    idx = np.random.permutation(T)[:J]
    idx2 = np.random.permutation(T)[:J]
    idx3 = np.random.permutation(C)[:J]
    idx4 = np.random.permutation(C)[:J]
    idx5 = np.random.permutation(D)[:J]
    idx6 = np.random.permutation(D)[:O]
    fk = mx_kscale(K)
    fr = mx_kscale(R)
    xtp = pack_weight(n((K, T)) / fk[:, None], "e2m1")
    wp = pack_weight(n((K, R)) * 1 / np.sqrt(K) * fk[:, None], "e4m3")
    w2p = pack_weight(n((K, R)) * 1 / np.sqrt(K) * fk[:, None], "e5m2")
    wbp = pack_weight(n((R, N)) * 1 / np.sqrt(R) / fr[:, None], "e2m1")
    return {
        "xt_words": xtp[0],
        "xt_scales": xtp[1],
        "w_words": wp[0],
        "w_scales": wp[1],
        "w2_words": w2p[0],
        "w2_scales": w2p[1],
        "sa": (sgn((R, 1))).astype(np.float32),
        "sb": (np.random.uniform(0.5, 1.6, (R, 1)) * fr[:, None]).astype(np.float32),
        "wb_words": wbp[0],
        "wb_scales": wbp[1],
        "offs": striped(idx),
        "offs2": striped(idx2),
        "offs3": striped(idx3),
        "offs4": striped(idx4),
        "offs5": striped(idx5),
        "offs6": striped(idx6),
    }


def reference(xt_words, xt_scales, w_words, w_scales, w2_words, w2_scales, sa, sb, wb_words, wb_scales, offs, offs2, offs3, offs4, offs5, offs6):
    idx = unstriped(offs)
    idx2 = unstriped(offs2)
    idx3 = unstriped(offs3)
    idx4 = unstriped(offs4)
    idx5 = unstriped(offs5)
    idx6 = unstriped(offs6)
    xtu = unpack_weight(xt_words, xt_scales, "e2m1")
    wu = unpack_weight(w_words, w_scales, "e4m3")
    w2u = unpack_weight(w2_words, w2_scales, "e5m2")
    wbu = unpack_weight(wb_words, wb_scales, "e2m1")
    xtidxg = xtu[:, idx]
    a = wu.T @ xtidxg
    xtidx2g = xtu[:, idx2]
    b = w2u.T @ xtidx2g
    pa = np.zeros((R, C))
    pa[:, idx3] = a * f64(sa)
    h1 = np.abs(pa[:, idx4] - b)
    pb = np.zeros((R, D))
    pb[:, idx5] = h1 * f64(sb)
    hid = pb[:, idx6]
    hidq = mxq(hid, 0, "e5m2")
    p = wbu.T @ hidq
    return p

@@ -1,0 +1,155 @@
+from contextlib import ExitStack
+
+import concourse.mybir as mybir
+
+F32 = mybir.dt.float32
+BF16 = mybir.dt.bfloat16
+I32 = mybir.dt.int32
+U32 = mybir.dt.uint32
+U16 = mybir.dt.uint16
+U8 = mybir.dt.uint8
+E4M3 = mybir.dt.float8_e4m3fn_x4
+E5M2 = mybir.dt.float8_e5m2_x4
+E2M1 = mybir.dt.float4_e2m1fn_x4
+COPY = mybir.ActivationFunctionType.Copy
+ALU = mybir.AluOpType
+
+P = 128
+PACK = 4
+QUADS = 4
+TOKENS, SLOTS, HIDDEN, BOARD, FEATURES = 2048, 256, 512, 512, 256
+K = 512
+FLOPS = 2 * K * HIDDEN * SLOTS * 2 + 2 * HIDDEN * FEATURES * SLOTS
+
+
+def tile_list_relayed_kernel(tc, xt_words, xt_scales, w_words, w_scales, w2_words, w2_scales, sa, sb,
+                                 wb_words, wb_scales, offs, offs2, offs3, offs4, offs5, offs6, out):
+    nc = tc.nc
+    with ExitStack() as ctx:
+        pool = ctx.enter_context(tc.tile_pool(name="held", bufs=1))
+        psum = ctx.enter_context(tc.psum_pool(name="psum", bufs=1))
+
+        def load_list(name, source):
+            tile = pool.tile([P, SLOTS // 16], U16, name=name)
+            nc.sync.dma_start(tile[:], source)
+            return tile
+
+        def cleared_plane(name, width):
+            plane = pool.tile([P, width], U8, name=name, align_bytes=64)
+            nc.vector.memset(plane[:].bitcast(I32), 0)
+            return plane
+
+        def load_scale_rows(queue, plane, scales):
+            rows = scales[0].bitcast(I32)
+            for r in range(4):
+                queue.dma_start(plane[r:P:32, :].bitcast(I32), rows[r:16:4, :])
+
+        def load_words(name, words):
+            tile = pool.tile([P, HIDDEN], U32, name=name)
+            nc.sync.dma_start(tile[:].bitcast(I32), words[0].rearrange("p c i -> p (c i)").bitcast(I32))
+            return tile
+
+        xt_plane = cleared_plane("xt_plane", TOKENS)
+        load_scale_rows(nc.scalar, xt_plane, xt_scales)
+        list1 = load_list("list1", offs)
+        w_rows = pool.tile([4, QUADS, HIDDEN // 4], I32, name="w_rows")
+        nc.sync.dma_start(w_rows[:], w_scales[0].bitcast(I32).rearrange("(q r) c -> r q c", r=4))
+        xt_table = pool.tile([P, TOKENS], U16, name="xt_table")
+        nc.sync.dma_start(xt_table[:].bitcast(I32), xt_words[0].bitcast(I32))
+        w_raw = load_words("w_raw", w_words)
+        list3 = load_list("list3", offs3)
+        sa_cols = pool.tile([P, PACK], F32, name="sa_cols")
+        nc.sync.dma_start(sa_cols[:], sa.rearrange("(p i) o -> p (i o)", i=PACK))
+        w2_raw = load_words("w2_raw", w2_words)
+        list2 = load_list("list2", offs2)
+
+        w_plane = cleared_plane("w_plane", HIDDEN)
+        boards_a = [pool.tile([P, BOARD], F32, name="board_a%d" % i) for i in range(PACK)]
+        for board in boards_a:
+            nc.vector.memset(board[:], 0.0)
+        w2_plane = cleared_plane("w2_plane", HIDDEN)
+        load_scale_rows(nc.sync, w2_plane, w2_scales)
+        list4 = load_list("list4", offs4)
+        sb_cols = pool.tile([P, PACK], F32, name="sb_cols")
+        nc.sync.dma_start(sb_cols[:], sb.rearrange("(p i) o -> p (i o)", i=PACK))
+        list5 = load_list("list5", offs5)
+        list6 = load_list("list6", offs6)
+        wb_codes = pool.tile([P, 2 * FEATURES], U8, name="wb_codes", align_bytes=64)
+        nc.sync.dma_start(wb_codes[:].bitcast(I32), wb_words[0].bitcast(I32))
+        wb_plane = cleared_plane("wb_plane", FEATURES)
+        load_scale_rows(nc.sync, wb_plane, wb_scales)
+
+        for q in range(QUADS):
+            nc.vector.tensor_copy(w_plane[32 * q : 32 * q + 4, :].bitcast(I32), w_rows[:, q, :])
+
+        def gather_tokens(name, offsets):
+            scales = pool.tile([P, SLOTS], U8, name=name + "_scales", align_bytes=64)
+            nc.vector.tensor_copy(scales[:], xt_plane[:].indirect(offsets[:]))
+            codes = pool.tile([P, SLOTS], U16, name=name + "_codes", align_bytes=64)
+            nc.vector.tensor_copy(codes[:], xt_table[:].indirect(offsets[:]))
+            return codes, scales
+
+        def dealt(source, i):
+            return source[:].rearrange("p (m i) -> p i m", i=PACK)[:, i, :]
+
+        w_codes = [pool.tile([P, P], U32, name="w_codes%d" % i, align_bytes=64) for i in range(PACK)]
+        w_dealt = [pool.tile([P, P], U8, name="w_dealt%d" % i, align_bytes=64) for i in range(PACK)]
+        nc.vector.tensor_copy(w_dealt[0][:], dealt(w_plane, 0))
+        x1_codes, x1_scales = gather_tokens("x1", list1)
+        for i in range(1, PACK):
+            nc.vector.tensor_copy(w_dealt[i][:], dealt(w_plane, i))
+        for i in range(PACK):
+            nc.scalar.copy(w_codes[i][:], dealt(w_raw, i))
+
+        a_rows = []
+        for i in range(PACK):
+            a_sum = psum.tile([P, SLOTS], F32, name="a_sum%d" % i)
+            nc.tensor.matmul_mx(a_sum[:], lhsT=w_codes[i][:].bitcast(E4M3), lhsT_scale=w_dealt[i][:],
+                                rhs=x1_codes[:].bitcast(E2M1), rhs_scale=x1_scales[:], start=True, stop=True)
+            rows = pool.tile([P, SLOTS], F32, name="a_rows%d" % i)
+            if i == 0:
+                nc.scalar.copy(rows[:], a_sum[:])
+            else:
+                nc.vector.tensor_copy(rows[:], a_sum[:])
+            a_rows.append(rows)
+        for i in range(PACK):
+            nc.scalar.activation(boards_a[i][:].indirect(list3[:]), a_rows[i][:], COPY, scale=sa_cols[:, i : i + 1])
+
+        x2_codes, x2_scales = gather_tokens("x2", list2)
+        w2_codes = pool.tile([P, PACK, P], U32, name="w2_codes", align_bytes=64)
+        nc.vector.tensor_copy(w2_codes[:], w2_raw[:].rearrange("p (m i) -> p i m", i=PACK))
+        w2_dealt = pool.tile([P, PACK, P], U8, name="w2_dealt", align_bytes=64)
+        nc.vector.tensor_copy(w2_dealt[:], w2_plane[:].rearrange("p (m i) -> p i m", i=PACK))
+        b_banks = [psum.tile([P, 2, SLOTS], F32, name="b_sum%d" % h) for h in range(2)]
+        for i in range(PACK):
+            nc.tensor.matmul_mx(b_banks[i // 2][:, i % 2, :], lhsT=w2_codes[:, i, :].bitcast(E5M2), lhsT_scale=w2_dealt[:, i, :],
+                                rhs=x2_codes[:].bitcast(E2M1), rhs_scale=x2_scales[:], start=True, stop=True)
+
+        boards_b = [pool.tile([P, BOARD], F32, name="board_b%d" % i) for i in range(PACK)]
+        hid = pool.tile([P, PACK * SLOTS], BF16, name="hid", align_bytes=64)
+        for i in range(PACK):
+            picked = pool.tile([P, SLOTS], F32, name="picked%d" % i)
+            nc.vector.tensor_copy(picked[:], boards_a[i][:].indirect(list4[:]))
+            diff = pool.tile([P, SLOTS], F32, name="diff%d" % i)
+            nc.vector.tensor_tensor(diff[:], picked[:], b_banks[i // 2][:, i % 2, :], ALU.subtract)
+            kept = pool.tile([P, SLOTS], F32, name="kept%d" % i)
+            nc.vector.scalar_tensor_tensor(kept[:], diff[:], -1.0, diff[:], ALU.mult, ALU.max)
+            nc.vector.memset(boards_b[i][:], 0.0)
+            nc.scalar.activation(boards_b[i][:].indirect(list5[:]), kept[:], COPY, scale=sb_cols[:, i : i + 1])
+        for i in range(PACK):
+            nc.scalar.activation(hid[:, i : PACK * SLOTS : PACK], boards_b[i][:].indirect(list6[:]), COPY)
+
+        hid_codes = pool.tile([P, SLOTS], U32, name="hid_codes", align_bytes=64)
+        hid_scales = pool.tile([P, SLOTS], U8, name="hid_scales", align_bytes=64)
+        nc.vector.quantize_mx(hid_codes[:].bitcast(E5M2), hid_scales[:], hid[:])
+        for h in range(FEATURES // P):
+            p_sum = psum.tile([P, SLOTS], F32, name="p_sum%d" % h)
+            nc.tensor.matmul_mx(p_sum[:], lhsT=wb_codes[:, 2 * P * h : 2 * P * (h + 1)].bitcast(E2M1), lhsT_scale=wb_plane[:, P * h : P * (h + 1)],
+                                rhs=hid_codes[:].bitcast(E5M2), rhs_scale=hid_scales[:], start=True, stop=True)
+            result = pool.tile([P, SLOTS], F32, name="result%d" % h)
+            if h == 0:
+                nc.scalar.copy(result[:], p_sum[:])
+                nc.scalar.dma_start(out[P * h : P * (h + 1), :], result[:])
+            else:
+                nc.vector.tensor_copy(result[:], p_sum[:])
+                nc.sync.dma_start(out[P * h : P * (h + 1), :], result[:])

@@ -49,6 +49,28 @@ def tile_list_relayed_kernel(tc, xt_words, xt_scales, w_words, w_scales, w2_word
             nc.sync.dma_start(tile[:].bitcast(I32), words[0].rearrange("p c i -> p (c i)").bitcast(I32))
             return tile
 
+        def load_row_weights(name, weights):
+            tile = pool.tile([P, PACK], F32, name=name)
+            nc.sync.dma_start(tile[:], weights.rearrange("(p i) o -> p (i o)", i=PACK))
+            return tile
+
+        def cleared_board(name, i):
+            board = pool.tile([P, BOARD], F32, name="%s%d" % (name, i), tag="board%d" % i)
+            nc.vector.memset(board[:], 0.0)
+            return board
+
+        def gather_tokens(name, offsets):
+            codes = pool.tile([P, SLOTS], U16, name=name + "_codes", tag="token_codes", align_bytes=64)
+            nc.vector.tensor_copy(codes[:], xt_table[:].indirect(offsets[:]))
+            scales = pool.tile([P, SLOTS], U8, name=name + "_scales", tag="token_scales", align_bytes=64)
+            nc.vector.tensor_copy(scales[:], xt_plane[:].indirect(offsets[:]))
+            return codes, scales
+
+        def deal(copy, name, kind, dtype, source, i):
+            tile = pool.tile([P, P], dtype, name="%s%d" % (name, i), tag="%s%d" % (kind, i), align_bytes=64)
+            copy(tile[:], source[:].rearrange("p (m i) -> p i m", i=PACK)[:, i, :])
+            return tile
+
         xt_plane = cleared_plane("xt_plane", TOKENS)
         load_scale_rows(nc.scalar, xt_plane, xt_scales)
         list1 = load_list("list1", offs)
@@ -58,20 +80,16 @@ def tile_list_relayed_kernel(tc, xt_words, xt_scales, w_words, w_scales, w2_word
         nc.sync.dma_start(xt_table[:].bitcast(I32), xt_words[0].bitcast(I32))
         w_raw = load_words("w_raw", w_words)
         list3 = load_list("list3", offs3)
-        sa_cols = pool.tile([P, PACK], F32, name="sa_cols")
-        nc.sync.dma_start(sa_cols[:], sa.rearrange("(p i) o -> p (i o)", i=PACK))
+        sa_cols = load_row_weights("sa_cols", sa)
         w2_raw = load_words("w2_raw", w2_words)
         list2 = load_list("list2", offs2)
 
         w_plane = cleared_plane("w_plane", HIDDEN)
-        boards_a = [pool.tile([P, BOARD], F32, name="board_a%d" % i) for i in range(PACK)]
-        for board in boards_a:
-            nc.vector.memset(board[:], 0.0)
         w2_plane = cleared_plane("w2_plane", HIDDEN)
         load_scale_rows(nc.sync, w2_plane, w2_scales)
+        boards_a = [cleared_board("board_a", i) for i in range(PACK)]
         list4 = load_list("list4", offs4)
-        sb_cols = pool.tile([P, PACK], F32, name="sb_cols")
-        nc.sync.dma_start(sb_cols[:], sb.rearrange("(p i) o -> p (i o)", i=PACK))
+        sb_cols = load_row_weights("sb_cols", sb)
         list5 = load_list("list5", offs5)
         list6 = load_list("list6", offs6)
         wb_codes = pool.tile([P, 2 * FEATURES], U8, name="wb_codes", align_bytes=64)
@@ -81,75 +99,59 @@ def tile_list_relayed_kernel(tc, xt_words, xt_scales, w_words, w_scales, w2_word
 
         for q in range(QUADS):
             nc.vector.tensor_copy(w_plane[32 * q : 32 * q + 4, :].bitcast(I32), w_rows[:, q, :])
-
-        def gather_tokens(name, offsets):
-            scales = pool.tile([P, SLOTS], U8, name=name + "_scales", align_bytes=64)
-            nc.vector.tensor_copy(scales[:], xt_plane[:].indirect(offsets[:]))
-            codes = pool.tile([P, SLOTS], U16, name=name + "_codes", align_bytes=64)
-            nc.vector.tensor_copy(codes[:], xt_table[:].indirect(offsets[:]))
-            return codes, scales
-
-        def dealt(source, i):
-            return source[:].rearrange("p (m i) -> p i m", i=PACK)[:, i, :]
-
-        w_codes = [pool.tile([P, P], U32, name="w_codes%d" % i, align_bytes=64) for i in range(PACK)]
-        w_dealt = [pool.tile([P, P], U8, name="w_dealt%d" % i, align_bytes=64) for i in range(PACK)]
-        nc.vector.tensor_copy(w_dealt[0][:], dealt(w_plane, 0))
+        w_dealt = [deal(nc.vector.tensor_copy, "w_dealt", "dealt_scales", U8, w_plane, 0)]
         x1_codes, x1_scales = gather_tokens("x1", list1)
         for i in range(1, PACK):
-            nc.vector.tensor_copy(w_dealt[i][:], dealt(w_plane, i))
-        for i in range(PACK):
-            nc.scalar.copy(w_codes[i][:], dealt(w_raw, i))
+            w_dealt.append(deal(nc.vector.tensor_copy, "w_dealt", "dealt_scales", U8, w_plane, i))
+        w_codes = [deal(nc.scalar.copy, "w_codes", "dealt_codes", U32, w_raw, i) for i in range(PACK)]
 
-        a_rows = []
         for i in range(PACK):
-            a_sum = psum.tile([P, SLOTS], F32, name="a_sum%d" % i)
+            a_sum = psum.tile([P, SLOTS], F32, name="a_sum%d" % i, tag="bank%d" % i)
             nc.tensor.matmul_mx(a_sum[:], lhsT=w_codes[i][:].bitcast(E4M3), lhsT_scale=w_dealt[i][:],
                                 rhs=x1_codes[:].bitcast(E2M1), rhs_scale=x1_scales[:], start=True, stop=True)
-            rows = pool.tile([P, SLOTS], F32, name="a_rows%d" % i)
+            a_rows = pool.tile([P, SLOTS], F32, name="a_rows%d" % i)
             if i == 0:
-                nc.scalar.copy(rows[:], a_sum[:])
+                nc.scalar.copy(a_rows[:], a_sum[:])
             else:
-                nc.vector.tensor_copy(rows[:], a_sum[:])
-            a_rows.append(rows)
-        for i in range(PACK):
-            nc.scalar.activation(boards_a[i][:].indirect(list3[:]), a_rows[i][:], COPY, scale=sa_cols[:, i : i + 1])
+                nc.vector.tensor_copy(a_rows[:], a_sum[:])
+            nc.scalar.activation(boards_a[i][:].indirect(list3[:]), a_rows[:], COPY, scale=sa_cols[:, i : i + 1])
 
         x2_codes, x2_scales = gather_tokens("x2", list2)
-        w2_codes = pool.tile([P, PACK, P], U32, name="w2_codes", align_bytes=64)
-        nc.vector.tensor_copy(w2_codes[:], w2_raw[:].rearrange("p (m i) -> p i m", i=PACK))
-        w2_dealt = pool.tile([P, PACK, P], U8, name="w2_dealt", align_bytes=64)
-        nc.vector.tensor_copy(w2_dealt[:], w2_plane[:].rearrange("p (m i) -> p i m", i=PACK))
-        b_banks = [psum.tile([P, 2, SLOTS], F32, name="b_sum%d" % h) for h in range(2)]
+        boards_b = []
         for i in range(PACK):
-            nc.tensor.matmul_mx(b_banks[i // 2][:, i % 2, :], lhsT=w2_codes[:, i, :].bitcast(E5M2), lhsT_scale=w2_dealt[:, i, :],
+            w2_codes = deal(nc.vector.tensor_copy, "w2_codes", "dealt_codes", U32, w2_raw, i)
+            w2_dealt = deal(nc.vector.tensor_copy, "w2_dealt", "dealt_scales", U8, w2_plane, i)
+            b_sum = psum.tile([P, SLOTS], F32, name="b_sum%d" % i)
+            nc.tensor.matmul_mx(b_sum[:], lhsT=w2_codes[:].bitcast(E5M2), lhsT_scale=w2_dealt[:],
                                 rhs=x2_codes[:].bitcast(E2M1), rhs_scale=x2_scales[:], start=True, stop=True)
-
-        boards_b = [pool.tile([P, BOARD], F32, name="board_b%d" % i) for i in range(PACK)]
-        hid = pool.tile([P, PACK * SLOTS], BF16, name="hid", align_bytes=64)
-        for i in range(PACK):
-            picked = pool.tile([P, SLOTS], F32, name="picked%d" % i)
-            nc.vector.tensor_copy(picked[:], boards_a[i][:].indirect(list4[:]))
+            b_rows = pool.tile([P, SLOTS], F32, name="b_rows%d" % i)
+            nc.vector.tensor_copy(b_rows[:], b_sum[:])
             diff = pool.tile([P, SLOTS], F32, name="diff%d" % i)
-            nc.vector.tensor_tensor(diff[:], picked[:], b_banks[i // 2][:, i % 2, :], ALU.subtract)
-            kept = pool.tile([P, SLOTS], F32, name="kept%d" % i)
+            nc.vector.tensor_tensor(diff[:], boards_a[i][:].indirect(list4[:]), b_rows[:], ALU.subtract)
+            kept = pool.tile([P, SLOTS], F32, name="kept%d" % i, tag="kept%d" % i, align_bytes=64)
             nc.vector.scalar_tensor_tensor(kept[:], diff[:], -1.0, diff[:], ALU.mult, ALU.max)
-            nc.vector.memset(boards_b[i][:], 0.0)
+            boards_b.append(cleared_board("board_b", i))
             nc.scalar.activation(boards_b[i][:].indirect(list5[:]), kept[:], COPY, scale=sb_cols[:, i : i + 1])
-        for i in range(PACK):
-            nc.scalar.activation(hid[:, i : PACK * SLOTS : PACK], boards_b[i][:].indirect(list6[:]), COPY)
 
-        hid_codes = pool.tile([P, SLOTS], U32, name="hid_codes", align_bytes=64)
-        hid_scales = pool.tile([P, SLOTS], U8, name="hid_scales", align_bytes=64)
-        nc.vector.quantize_mx(hid_codes[:].bitcast(E5M2), hid_scales[:], hid[:])
-        for h in range(FEATURES // P):
-            p_sum = psum.tile([P, SLOTS], F32, name="p_sum%d" % h)
-            nc.tensor.matmul_mx(p_sum[:], lhsT=wb_codes[:, 2 * P * h : 2 * P * (h + 1)].bitcast(E2M1), lhsT_scale=wb_plane[:, P * h : P * (h + 1)],
-                                rhs=hid_codes[:].bitcast(E5M2), rhs_scale=hid_scales[:], start=True, stop=True)
-            result = pool.tile([P, SLOTS], F32, name="result%d" % h)
-            if h == 0:
-                nc.scalar.copy(result[:], p_sum[:])
-                nc.scalar.dma_start(out[P * h : P * (h + 1), :], result[:])
-            else:
-                nc.vector.tensor_copy(result[:], p_sum[:])
-                nc.sync.dma_start(out[P * h : P * (h + 1), :], result[:])
+        half = SLOTS // 2
+        out_halves = out.rearrange("(h p) o -> h p o", p=P)
+        for part in range(2):
+            tag = "hid0" if part == 0 else "kept%d" % (PACK - 1)
+            hid = pool.tile([P, PACK * half], BF16, name="hid%d" % part, tag=tag, align_bytes=64)
+            offsets = list6[:, part * half // 16 : (part + 1) * half // 16]
+            for i in range(PACK):
+                nc.scalar.activation(hid[:, i : PACK * half : PACK], boards_b[i][:].indirect(offsets), COPY)
+            hid_codes = pool.tile([P, half], U32, name="hid_codes%d" % part, align_bytes=64)
+            hid_scales = pool.tile([P, half], U8, name="hid_scales%d" % part, align_bytes=64)
+            nc.vector.quantize_mx(hid_codes[:].bitcast(E5M2), hid_scales[:], hid[:])
+            for h in range(FEATURES // P):
+                p_sum = psum.tile([P, half], F32, name="p_sum%d%d" % (part, h), tag="bank%d" % (2 * part + h))
+                nc.tensor.matmul_mx(p_sum[:], lhsT=wb_codes[:, 2 * P * h : 2 * P * (h + 1)].bitcast(E2M1), lhsT_scale=wb_plane[:, P * h : P * (h + 1)],
+                                    rhs=hid_codes[:].bitcast(E5M2), rhs_scale=hid_scales[:], start=True, stop=True)
+                result = pool.tile([P, half], F32, name="result%d%d" % (part, h))
+                if part == 1 and h == 0:
+                    nc.scalar.copy(result[:], p_sum[:])
+                    nc.scalar.dma_start(out_halves[h, :, part * half : (part + 1) * half], result[:])
+                else:
+                    nc.vector.tensor_copy(result[:], p_sum[:])
+                    nc.sync.dma_start(out_halves[h, :, part * half : (part + 1) * half], result[:])

@@ -27,6 +27,7 @@ def tile_list_relayed_kernel(tc, xt_words, xt_scales, w_words, w_scales, w2_word
     nc = tc.nc
     with ExitStack() as ctx:
         pool = ctx.enter_context(tc.tile_pool(name="held", bufs=1))
+        tail = ctx.enter_context(tc.tile_pool(name="tail", bufs=1))
         psum = ctx.enter_context(tc.psum_pool(name="psum", bufs=1))
 
         def load_list(name, source):
@@ -34,8 +35,8 @@ def tile_list_relayed_kernel(tc, xt_words, xt_scales, w_words, w_scales, w2_word
             nc.sync.dma_start(tile[:], source)
             return tile
 
-        def cleared_plane(name, width):
-            plane = pool.tile([P, width], U8, name=name, align_bytes=64)
+        def cleared_plane(name, width, tag):
+            plane = pool.tile([P, width], U8, name=name, tag=tag, align_bytes=64)
             nc.vector.memset(plane[:].bitcast(I32), 0)
             return plane
 
@@ -44,8 +45,8 @@ def tile_list_relayed_kernel(tc, xt_words, xt_scales, w_words, w_scales, w2_word
             for r in range(4):
                 queue.dma_start(plane[r:P:32, :].bitcast(I32), rows[r:16:4, :])
 
-        def load_words(name, words):
-            tile = pool.tile([P, HIDDEN], U32, name=name)
+        def load_words(name, words, tag):
+            tile = pool.tile([P, HIDDEN], U32, name=name, tag=tag, align_bytes=64)
             nc.sync.dma_start(tile[:].bitcast(I32), words[0].rearrange("p c i -> p (c i)").bitcast(I32))
             return tile
 
@@ -54,90 +55,100 @@ def tile_list_relayed_kernel(tc, xt_words, xt_scales, w_words, w_scales, w2_word
             nc.sync.dma_start(tile[:], weights.rearrange("(p i) o -> p (i o)", i=PACK))
             return tile
 
-        def cleared_board(name, i):
-            board = pool.tile([P, BOARD], F32, name="%s%d" % (name, i), tag="board%d" % i)
-            nc.vector.memset(board[:], 0.0)
+        def cleared_board(engine, name, i):
+            board = pool.tile([P, BOARD], F32, name="%s%d" % (name, i), tag="board%d" % i, align_bytes=64)
+            engine.memset(board[:], 0.0)
             return board
 
-        def gather_tokens(name, offsets):
-            codes = pool.tile([P, SLOTS], U16, name=name + "_codes", tag="token_codes", align_bytes=64)
+        def gather_tokens(name, offsets, codes_tag):
+            codes = pool.tile([P, SLOTS], U16, name=name + "_codes", tag=codes_tag, align_bytes=64)
             nc.vector.tensor_copy(codes[:], xt_table[:].indirect(offsets[:]))
             scales = pool.tile([P, SLOTS], U8, name=name + "_scales", tag="token_scales", align_bytes=64)
             nc.vector.tensor_copy(scales[:], xt_plane[:].indirect(offsets[:]))
             return codes, scales
 
-        def deal(copy, name, kind, dtype, source, i):
-            tile = pool.tile([P, P], dtype, name="%s%d" % (name, i), tag="%s%d" % (kind, i), align_bytes=64)
-            copy(tile[:], source[:].rearrange("p (m i) -> p i m", i=PACK)[:, i, :])
-            return tile
-
-        xt_plane = cleared_plane("xt_plane", TOKENS)
-        load_scale_rows(nc.scalar, xt_plane, xt_scales)
+        xt_plane = cleared_plane("xt_plane", TOKENS, "xt_plane")
         list1 = load_list("list1", offs)
         w_rows = pool.tile([4, QUADS, HIDDEN // 4], I32, name="w_rows")
         nc.sync.dma_start(w_rows[:], w_scales[0].bitcast(I32).rearrange("(q r) c -> r q c", r=4))
+        load_scale_rows(nc.scalar, xt_plane, xt_scales)
         xt_table = pool.tile([P, TOKENS], U16, name="xt_table")
         nc.sync.dma_start(xt_table[:].bitcast(I32), xt_words[0].bitcast(I32))
-        w_raw = load_words("w_raw", w_words)
+        w_raw = load_words("w_raw", w_words, "board2")
         list3 = load_list("list3", offs3)
         sa_cols = load_row_weights("sa_cols", sa)
-        w2_raw = load_words("w2_raw", w2_words)
+        w2_raw = load_words("w2_raw", w2_words, "w2_raw")
         list2 = load_list("list2", offs2)
 
-        w_plane = cleared_plane("w_plane", HIDDEN)
-        w2_plane = cleared_plane("w2_plane", HIDDEN)
+        w_plane = cleared_plane("w_plane", HIDDEN, "board3")
+        w2_plane = cleared_plane("w2_plane", HIDDEN, "w2_plane")
         load_scale_rows(nc.sync, w2_plane, w2_scales)
-        boards_a = [cleared_board("board_a", i) for i in range(PACK)]
+        boards_a = [cleared_board(nc.vector, "board_a", i) for i in range(2)]
         list4 = load_list("list4", offs4)
         sb_cols = load_row_weights("sb_cols", sb)
         list5 = load_list("list5", offs5)
         list6 = load_list("list6", offs6)
         wb_codes = pool.tile([P, 2 * FEATURES], U8, name="wb_codes", align_bytes=64)
         nc.sync.dma_start(wb_codes[:].bitcast(I32), wb_words[0].bitcast(I32))
-        wb_plane = cleared_plane("wb_plane", FEATURES)
+        wb_plane = cleared_plane("wb_plane", FEATURES, "wb_plane")
         load_scale_rows(nc.sync, wb_plane, wb_scales)
 
         for q in range(QUADS):
             nc.vector.tensor_copy(w_plane[32 * q : 32 * q + 4, :].bitcast(I32), w_rows[:, q, :])
-        w_dealt = [deal(nc.vector.tensor_copy, "w_dealt", "dealt_scales", U8, w_plane, 0)]
-        x1_codes, x1_scales = gather_tokens("x1", list1)
-        for i in range(1, PACK):
-            w_dealt.append(deal(nc.vector.tensor_copy, "w_dealt", "dealt_scales", U8, w_plane, i))
-        w_codes = [deal(nc.scalar.copy, "w_codes", "dealt_codes", U32, w_raw, i) for i in range(PACK)]
+        w_plane_by_slice = w_plane[:].rearrange("p (m i) -> p i m", i=PACK)
+        w_raw_by_column = w_raw[:].rearrange("p (m i) -> p m i", i=PACK)
+        first_scales = pool.tile([P, P], U8, name="first_scales", tag="dealt_scales", align_bytes=64)
+        nc.vector.tensor_copy(first_scales[:], w_plane_by_slice[:, 0, :])
+        x1_codes, x1_scales = gather_tokens("x1", list1, "x1_codes")
+        first_codes = pool.tile([P, P], U32, name="first_codes", tag="first_codes", align_bytes=64)
+        nc.scalar.copy(first_codes[:], w_raw_by_column[:, :, 0])
+        later_codes = pool.tile([P, PACK - 1, P], U32, name="later_codes", tag="dealt_codes", align_bytes=64)
+        nc.scalar.copy(later_codes[:].rearrange("p i m -> p m i"), w_raw_by_column[:, :, 1:PACK])
+        w_codes = [first_codes[:]] + [later_codes[:, i, :] for i in range(PACK - 1)]
+        w_dealt = [first_scales[:]]
 
         for i in range(PACK):
             a_sum = psum.tile([P, SLOTS], F32, name="a_sum%d" % i, tag="bank%d" % i)
-            nc.tensor.matmul_mx(a_sum[:], lhsT=w_codes[i][:].bitcast(E4M3), lhsT_scale=w_dealt[i][:],
+            nc.tensor.matmul_mx(a_sum[:], lhsT=w_codes[i].bitcast(E4M3), lhsT_scale=w_dealt[i],
                                 rhs=x1_codes[:].bitcast(E2M1), rhs_scale=x1_scales[:], start=True, stop=True)
             a_rows = pool.tile([P, SLOTS], F32, name="a_rows%d" % i)
             if i == 0:
                 nc.scalar.copy(a_rows[:], a_sum[:])
+                later_scales = pool.tile([P, PACK - 1, P], U8, name="later_scales", tag="dealt_scales", align_bytes=64)
+                nc.vector.tensor_copy(later_scales[:], w_plane_by_slice[:, 1:PACK, :])
+                w_dealt.extend(later_scales[:, s, :] for s in range(PACK - 1))
             else:
                 nc.vector.tensor_copy(a_rows[:], a_sum[:])
+            if i >= 2:
+                boards_a.append(cleared_board(nc.gpsimd, "board_a", i))
             nc.scalar.activation(boards_a[i][:].indirect(list3[:]), a_rows[:], COPY, scale=sa_cols[:, i : i + 1])
 
-        x2_codes, x2_scales = gather_tokens("x2", list2)
+        x2_codes, x2_scales = gather_tokens("x2", list2, "first_codes")
+        w2_codes = pool.tile([P, PACK, P], U32, name="w2_codes", tag="dealt_codes", align_bytes=64)
+        nc.vector.tensor_copy(w2_codes[:].rearrange("p i m -> p m i"), w2_raw[:].rearrange("p (m i) -> p m i", i=PACK))
+        w2_dealt = pool.tile([P, PACK, P], U8, name="w2_dealt", tag="dealt_scales", align_bytes=64)
+        nc.vector.tensor_copy(w2_dealt[:], w2_plane[:].rearrange("p (m i) -> p i m", i=PACK))
         boards_b = []
         for i in range(PACK):
-            w2_codes = deal(nc.vector.tensor_copy, "w2_codes", "dealt_codes", U32, w2_raw, i)
-            w2_dealt = deal(nc.vector.tensor_copy, "w2_dealt", "dealt_scales", U8, w2_plane, i)
             b_sum = psum.tile([P, SLOTS], F32, name="b_sum%d" % i)
-            nc.tensor.matmul_mx(b_sum[:], lhsT=w2_codes[:].bitcast(E5M2), lhsT_scale=w2_dealt[:],
+            nc.tensor.matmul_mx(b_sum[:], lhsT=w2_codes[:, i, :].bitcast(E5M2), lhsT_scale=w2_dealt[:, i, :],
                                 rhs=x2_codes[:].bitcast(E2M1), rhs_scale=x2_scales[:], start=True, stop=True)
             b_rows = pool.tile([P, SLOTS], F32, name="b_rows%d" % i)
             nc.vector.tensor_copy(b_rows[:], b_sum[:])
             diff = pool.tile([P, SLOTS], F32, name="diff%d" % i)
             nc.vector.tensor_tensor(diff[:], boards_a[i][:].indirect(list4[:]), b_rows[:], ALU.subtract)
-            kept = pool.tile([P, SLOTS], F32, name="kept%d" % i, tag="kept%d" % i, align_bytes=64)
+            if i == PACK - 1:
+                kept = tail.tile([P, SLOTS], F32, name="kept%d" % i, offset=512, align_bytes=64)
+            else:
+                kept = pool.tile([P, SLOTS], F32, name="kept%d" % i)
             nc.vector.scalar_tensor_tensor(kept[:], diff[:], -1.0, diff[:], ALU.mult, ALU.max)
-            boards_b.append(cleared_board("board_b", i))
+            boards_b.append(cleared_board(nc.gpsimd, "board_b", i))
             nc.scalar.activation(boards_b[i][:].indirect(list5[:]), kept[:], COPY, scale=sb_cols[:, i : i + 1])
 
         half = SLOTS // 2
         out_halves = out.rearrange("(h p) o -> h p o", p=P)
         for part in range(2):
-            tag = "hid0" if part == 0 else "kept%d" % (PACK - 1)
-            hid = pool.tile([P, PACK * half], BF16, name="hid%d" % part, tag=tag, align_bytes=64)
+            hid = tail.tile([P, PACK * half], BF16, name="hid%d" % part, offset=1024 * part, align_bytes=64)
             offsets = list6[:, part * half // 16 : (part + 1) * half // 16]
             for i in range(PACK):
                 nc.scalar.activation(hid[:, i : PACK * half : PACK], boards_b[i][:].indirect(offsets), COPY)

@@ -133,10 +133,10 @@ def tile_list_relayed_kernel(tc, xt_words, xt_scales, w_words, w_scales, w2_word
             b_sum = psum.tile([P, SLOTS], F32, name="b_sum%d" % i)
             nc.tensor.matmul_mx(b_sum[:], lhsT=w2_codes[:, i, :].bitcast(E5M2), lhsT_scale=w2_dealt[:, i, :],
                                 rhs=x2_codes[:].bitcast(E2M1), rhs_scale=x2_scales[:], start=True, stop=True)
-            b_rows = pool.tile([P, SLOTS], F32, name="b_rows%d" % i)
-            nc.vector.tensor_copy(b_rows[:], b_sum[:])
+            picked = pool.tile([P, SLOTS], F32, name="picked%d" % i, tag=("w2_raw", "w2_plane")[i % 2], align_bytes=64)
+            nc.vector.tensor_copy(picked[:], boards_a[i][:].indirect(list4[:]))
             diff = pool.tile([P, SLOTS], F32, name="diff%d" % i)
-            nc.vector.tensor_tensor(diff[:], boards_a[i][:].indirect(list4[:]), b_rows[:], ALU.subtract)
+            nc.vector.tensor_tensor(diff[:], picked[:], b_sum[:], ALU.subtract)
             if i == PACK - 1:
                 kept = tail.tile([P, SLOTS], F32, name="kept%d" % i, offset=512, align_bytes=64)
             else:

@@ -16,10 +16,19 @@ ALU = mybir.AluOpType
 
 P = 128
 PACK = 4
-QUADS = 4
-TOKENS, SLOTS, HIDDEN, BOARD, FEATURES = 2048, 256, 512, 512, 256
-K = 512
-FLOPS = 2 * K * HIDDEN * SLOTS * 2 + 2 * HIDDEN * FEATURES * SLOTS
+QUADRANTS = 4
+QUADRANT = P // QUADRANTS
+LIVE_ROWS = 4
+LIST_ROWS = 16
+E2M1_BYTES = 2
+MX_ALIGN = 64
+K, TOKENS, SLOTS, HIDDEN, BOARD, FEATURES = 512, 2048, 256, 512, 512, 256
+EARLY_BOARDS = 2
+PARTS = 2
+PART = SLOTS // PARTS
+PART_BYTES = 2 * PACK * PART
+
+FLOPS = 2 * (2 * K * HIDDEN * SLOTS) + 2 * HIDDEN * FEATURES * SLOTS
 
 
 def tile_list_relayed_kernel(tc, xt_words, xt_scales, w_words, w_scales, w2_words, w2_scales, sa, sb,
@@ -31,22 +40,22 @@ def tile_list_relayed_kernel(tc, xt_words, xt_scales, w_words, w_scales, w2_word
         psum = ctx.enter_context(tc.psum_pool(name="psum", bufs=1))
 
         def load_list(name, source):
-            tile = pool.tile([P, SLOTS // 16], U16, name=name)
+            tile = pool.tile([P, SLOTS // LIST_ROWS], U16, name=name)
             nc.sync.dma_start(tile[:], source)
             return tile
 
         def cleared_plane(name, width, tag):
-            plane = pool.tile([P, width], U8, name=name, tag=tag, align_bytes=64)
+            plane = pool.tile([P, width], U8, name=name, tag=tag, align_bytes=MX_ALIGN)
             nc.vector.memset(plane[:].bitcast(I32), 0)
             return plane
 
         def load_scale_rows(queue, plane, scales):
             rows = scales[0].bitcast(I32)
-            for r in range(4):
-                queue.dma_start(plane[r:P:32, :].bitcast(I32), rows[r:16:4, :])
+            for u in range(LIVE_ROWS):
+                queue.dma_start(plane[u:P:QUADRANT, :].bitcast(I32), rows[u : QUADRANTS * LIVE_ROWS : LIVE_ROWS, :])
 
         def load_words(name, words, tag):
-            tile = pool.tile([P, HIDDEN], U32, name=name, tag=tag, align_bytes=64)
+            tile = pool.tile([P, HIDDEN], U32, name=name, tag=tag, align_bytes=MX_ALIGN)
             nc.sync.dma_start(tile[:].bitcast(I32), words[0].rearrange("p c i -> p (c i)").bitcast(I32))
             return tile
 
@@ -56,21 +65,21 @@ def tile_list_relayed_kernel(tc, xt_words, xt_scales, w_words, w_scales, w2_word
             return tile
 
         def cleared_board(engine, name, i):
-            board = pool.tile([P, BOARD], F32, name="%s%d" % (name, i), tag="board%d" % i, align_bytes=64)
+            board = pool.tile([P, BOARD], F32, name="%s%d" % (name, i), tag="board%d" % i, align_bytes=MX_ALIGN)
             engine.memset(board[:], 0.0)
             return board
 
         def gather_tokens(name, offsets, codes_tag):
-            codes = pool.tile([P, SLOTS], U16, name=name + "_codes", tag=codes_tag, align_bytes=64)
+            codes = pool.tile([P, SLOTS], U16, name=name + "_codes", tag=codes_tag, align_bytes=MX_ALIGN)
             nc.vector.tensor_copy(codes[:], xt_table[:].indirect(offsets[:]))
-            scales = pool.tile([P, SLOTS], U8, name=name + "_scales", tag="token_scales", align_bytes=64)
+            scales = pool.tile([P, SLOTS], U8, name=name + "_scales", tag="token_scales", align_bytes=MX_ALIGN)
             nc.vector.tensor_copy(scales[:], xt_plane[:].indirect(offsets[:]))
             return codes, scales
 
         xt_plane = cleared_plane("xt_plane", TOKENS, "xt_plane")
         list1 = load_list("list1", offs)
-        w_rows = pool.tile([4, QUADS, HIDDEN // 4], I32, name="w_rows")
-        nc.sync.dma_start(w_rows[:], w_scales[0].bitcast(I32).rearrange("(q r) c -> r q c", r=4))
+        w_staged = pool.tile([LIVE_ROWS, QUADRANTS, HIDDEN // 4], I32, name="w_staged")
+        nc.sync.dma_start(w_staged[:], w_scales[0].bitcast(I32).rearrange("(q u) c -> u q c", u=LIVE_ROWS))
         load_scale_rows(nc.scalar, xt_plane, xt_scales)
         xt_table = pool.tile([P, TOKENS], U16, name="xt_table")
         nc.sync.dma_start(xt_table[:].bitcast(I32), xt_words[0].bitcast(I32))
@@ -83,86 +92,88 @@ def tile_list_relayed_kernel(tc, xt_words, xt_scales, w_words, w_scales, w2_word
         w_plane = cleared_plane("w_plane", HIDDEN, "board3")
         w2_plane = cleared_plane("w2_plane", HIDDEN, "w2_plane")
         load_scale_rows(nc.sync, w2_plane, w2_scales)
-        boards_a = [cleared_board(nc.vector, "board_a", i) for i in range(2)]
+        boards_a = [cleared_board(nc.vector, "board_a", i) for i in range(EARLY_BOARDS)]
         list4 = load_list("list4", offs4)
         sb_cols = load_row_weights("sb_cols", sb)
         list5 = load_list("list5", offs5)
         list6 = load_list("list6", offs6)
-        wb_codes = pool.tile([P, 2 * FEATURES], U8, name="wb_codes", align_bytes=64)
+        wb_codes = pool.tile([P, E2M1_BYTES * FEATURES], U8, name="wb_codes", align_bytes=MX_ALIGN)
         nc.sync.dma_start(wb_codes[:].bitcast(I32), wb_words[0].bitcast(I32))
         wb_plane = cleared_plane("wb_plane", FEATURES, "wb_plane")
         load_scale_rows(nc.sync, wb_plane, wb_scales)
 
-        for q in range(QUADS):
-            nc.vector.tensor_copy(w_plane[32 * q : 32 * q + 4, :].bitcast(I32), w_rows[:, q, :])
+        for q in range(QUADRANTS):
+            nc.vector.tensor_copy(w_plane[QUADRANT * q : QUADRANT * q + LIVE_ROWS, :].bitcast(I32), w_staged[:, q, :])
         w_plane_by_slice = w_plane[:].rearrange("p (m i) -> p i m", i=PACK)
         w_raw_by_column = w_raw[:].rearrange("p (m i) -> p m i", i=PACK)
-        first_scales = pool.tile([P, P], U8, name="first_scales", tag="dealt_scales", align_bytes=64)
+        first_scales = pool.tile([P, P], U8, name="first_scales", tag="dealt_scales", align_bytes=MX_ALIGN)
         nc.vector.tensor_copy(first_scales[:], w_plane_by_slice[:, 0, :])
         x1_codes, x1_scales = gather_tokens("x1", list1, "x1_codes")
-        first_codes = pool.tile([P, P], U32, name="first_codes", tag="first_codes", align_bytes=64)
+        first_codes = pool.tile([P, P], U32, name="first_codes", tag="first_codes", align_bytes=MX_ALIGN)
         nc.scalar.copy(first_codes[:], w_raw_by_column[:, :, 0])
-        later_codes = pool.tile([P, PACK - 1, P], U32, name="later_codes", tag="dealt_codes", align_bytes=64)
+        later_codes = pool.tile([P, PACK - 1, P], U32, name="later_codes", tag="dealt_codes", align_bytes=MX_ALIGN)
         nc.scalar.copy(later_codes[:].rearrange("p i m -> p m i"), w_raw_by_column[:, :, 1:PACK])
         w_codes = [first_codes[:]] + [later_codes[:, i, :] for i in range(PACK - 1)]
-        w_dealt = [first_scales[:]]
+        w_dealt_scales = [first_scales[:]]
 
         for i in range(PACK):
             a_sum = psum.tile([P, SLOTS], F32, name="a_sum%d" % i, tag="bank%d" % i)
-            nc.tensor.matmul_mx(a_sum[:], lhsT=w_codes[i].bitcast(E4M3), lhsT_scale=w_dealt[i],
+            nc.tensor.matmul_mx(a_sum[:], lhsT=w_codes[i].bitcast(E4M3), lhsT_scale=w_dealt_scales[i],
                                 rhs=x1_codes[:].bitcast(E2M1), rhs_scale=x1_scales[:], start=True, stop=True)
             a_rows = pool.tile([P, SLOTS], F32, name="a_rows%d" % i)
             if i == 0:
                 nc.scalar.copy(a_rows[:], a_sum[:])
-                later_scales = pool.tile([P, PACK - 1, P], U8, name="later_scales", tag="dealt_scales", align_bytes=64)
+                later_scales = pool.tile([P, PACK - 1, P], U8, name="later_scales", tag="dealt_scales", align_bytes=MX_ALIGN)
                 nc.vector.tensor_copy(later_scales[:], w_plane_by_slice[:, 1:PACK, :])
-                w_dealt.extend(later_scales[:, s, :] for s in range(PACK - 1))
+                w_dealt_scales.extend(later_scales[:, later, :] for later in range(PACK - 1))
             else:
                 nc.vector.tensor_copy(a_rows[:], a_sum[:])
-            if i >= 2:
+            if i >= EARLY_BOARDS:
                 boards_a.append(cleared_board(nc.gpsimd, "board_a", i))
             nc.scalar.activation(boards_a[i][:].indirect(list3[:]), a_rows[:], COPY, scale=sa_cols[:, i : i + 1])
 
         x2_codes, x2_scales = gather_tokens("x2", list2, "first_codes")
-        w2_codes = pool.tile([P, PACK, P], U32, name="w2_codes", tag="dealt_codes", align_bytes=64)
+        w2_codes = pool.tile([P, PACK, P], U32, name="w2_codes", tag="dealt_codes", align_bytes=MX_ALIGN)
         nc.vector.tensor_copy(w2_codes[:].rearrange("p i m -> p m i"), w2_raw[:].rearrange("p (m i) -> p m i", i=PACK))
-        w2_dealt = pool.tile([P, PACK, P], U8, name="w2_dealt", tag="dealt_scales", align_bytes=64)
-        nc.vector.tensor_copy(w2_dealt[:], w2_plane[:].rearrange("p (m i) -> p i m", i=PACK))
+        w2_dealt_scales = pool.tile([P, PACK, P], U8, name="w2_dealt_scales", tag="dealt_scales", align_bytes=MX_ALIGN)
+        nc.vector.tensor_copy(w2_dealt_scales[:], w2_plane[:].rearrange("p (m i) -> p i m", i=PACK))
+
         boards_b = []
         for i in range(PACK):
             b_sum = psum.tile([P, SLOTS], F32, name="b_sum%d" % i)
-            nc.tensor.matmul_mx(b_sum[:], lhsT=w2_codes[:, i, :].bitcast(E5M2), lhsT_scale=w2_dealt[:, i, :],
+            nc.tensor.matmul_mx(b_sum[:], lhsT=w2_codes[:, i, :].bitcast(E5M2), lhsT_scale=w2_dealt_scales[:, i, :],
                                 rhs=x2_codes[:].bitcast(E2M1), rhs_scale=x2_scales[:], start=True, stop=True)
-            picked = pool.tile([P, SLOTS], F32, name="picked%d" % i, tag=("w2_raw", "w2_plane")[i % 2], align_bytes=64)
+            picked = pool.tile([P, SLOTS], F32, name="picked%d" % i, tag=("w2_raw", "w2_plane")[i % 2], align_bytes=MX_ALIGN)
             nc.vector.tensor_copy(picked[:], boards_a[i][:].indirect(list4[:]))
-            diff = pool.tile([P, SLOTS], F32, name="diff%d" % i)
-            nc.vector.tensor_tensor(diff[:], picked[:], b_sum[:], ALU.subtract)
             if i == PACK - 1:
-                kept = tail.tile([P, SLOTS], F32, name="kept%d" % i, offset=512, align_bytes=64)
+                diff = tail.tile([P, SLOTS], F32, name="diff%d" % i, offset=PART_BYTES // 2, align_bytes=MX_ALIGN)
             else:
-                kept = pool.tile([P, SLOTS], F32, name="kept%d" % i)
-            nc.vector.scalar_tensor_tensor(kept[:], diff[:], -1.0, diff[:], ALU.mult, ALU.max)
+                diff = pool.tile([P, SLOTS], F32, name="diff%d" % i)
+            nc.vector.tensor_tensor(diff[:], picked[:], b_sum[:], ALU.subtract)
+            h1 = pool.tile([P, SLOTS], F32, name="h1_%d" % i)
+            nc.vector.scalar_tensor_tensor(h1[:], diff[:], -1.0, diff[:], ALU.mult, ALU.max)
             boards_b.append(cleared_board(nc.gpsimd, "board_b", i))
-            nc.scalar.activation(boards_b[i][:].indirect(list5[:]), kept[:], COPY, scale=sb_cols[:, i : i + 1])
+            nc.scalar.activation(boards_b[i][:].indirect(list5[:]), h1[:], COPY, scale=sb_cols[:, i : i + 1])
 
-        half = SLOTS // 2
-        out_halves = out.rearrange("(h p) o -> h p o", p=P)
-        for part in range(2):
-            hid = tail.tile([P, PACK * half], BF16, name="hid%d" % part, offset=1024 * part, align_bytes=64)
-            offsets = list6[:, part * half // 16 : (part + 1) * half // 16]
+        out_rows = out.rearrange("(h p) o -> h p o", p=P)
+        for part in range(PARTS):
+            places = slice(part * PART, (part + 1) * PART)
+            hid = tail.tile([P, PACK * PART], BF16, name="hid%d" % part, offset=PART_BYTES * part, align_bytes=MX_ALIGN)
+            offsets = list6[:, part * PART // LIST_ROWS : (part + 1) * PART // LIST_ROWS]
             for i in range(PACK):
-                nc.scalar.activation(hid[:, i : PACK * half : PACK], boards_b[i][:].indirect(offsets), COPY)
-            hid_codes = pool.tile([P, half], U32, name="hid_codes%d" % part, align_bytes=64)
-            hid_scales = pool.tile([P, half], U8, name="hid_scales%d" % part, align_bytes=64)
+                nc.scalar.activation(hid[:, i : PACK * PART : PACK], boards_b[i][:].indirect(offsets), COPY)
+            hid_codes = pool.tile([P, PART], U32, name="hid_codes%d" % part, align_bytes=MX_ALIGN)
+            hid_scales = pool.tile([P, PART], U8, name="hid_scales%d" % part, align_bytes=MX_ALIGN)
             nc.vector.quantize_mx(hid_codes[:].bitcast(E5M2), hid_scales[:], hid[:])
             for h in range(FEATURES // P):
-                p_sum = psum.tile([P, half], F32, name="p_sum%d%d" % (part, h), tag="bank%d" % (2 * part + h))
-                nc.tensor.matmul_mx(p_sum[:], lhsT=wb_codes[:, 2 * P * h : 2 * P * (h + 1)].bitcast(E2M1), lhsT_scale=wb_plane[:, P * h : P * (h + 1)],
+                out_sum = psum.tile([P, PART], F32, name="out_sum%d%d" % (part, h), tag="bank%d" % (FEATURES // P * part + h))
+                nc.tensor.matmul_mx(out_sum[:], lhsT=wb_codes[:, E2M1_BYTES * P * h : E2M1_BYTES * P * (h + 1)].bitcast(E2M1),
+                                    lhsT_scale=wb_plane[:, P * h : P * (h + 1)],
                                     rhs=hid_codes[:].bitcast(E5M2), rhs_scale=hid_scales[:], start=True, stop=True)
-                result = pool.tile([P, half], F32, name="result%d%d" % (part, h))
-                if part == 1 and h == 0:
-                    nc.scalar.copy(result[:], p_sum[:])
-                    nc.scalar.dma_start(out_halves[h, :, part * half : (part + 1) * half], result[:])
+                result = pool.tile([P, PART], F32, name="result%d%d" % (part, h))
+                if part == PARTS - 1 and h == 0:
+                    nc.scalar.copy(result[:], out_sum[:])
+                    nc.scalar.dma_start(out_rows[h, :, places], result[:])
                 else:
-                    nc.vector.tensor_copy(result[:], p_sum[:])
-                    nc.sync.dma_start(out_halves[h, :, part * half : (part + 1) * half], result[:])
+                    nc.vector.tensor_copy(result[:], out_sum[:])
+                    nc.sync.dma_start(out_rows[h, :, places], result[:])

from contextlib import ExitStack

import concourse.mybir as mybir

F32 = mybir.dt.float32
BF16 = mybir.dt.bfloat16
I32 = mybir.dt.int32
U32 = mybir.dt.uint32
U16 = mybir.dt.uint16
U8 = mybir.dt.uint8
E4M3 = mybir.dt.float8_e4m3fn_x4
E5M2 = mybir.dt.float8_e5m2_x4
E2M1 = mybir.dt.float4_e2m1fn_x4
COPY = mybir.ActivationFunctionType.Copy
ALU = mybir.AluOpType

P = 128
PACK = 4
QUADRANTS = 4
QUADRANT = P // QUADRANTS
LIVE_ROWS = 4
LIST_ROWS = 16
E2M1_BYTES = 2
MX_ALIGN = 64
K, TOKENS, SLOTS, HIDDEN, BOARD, FEATURES = 512, 2048, 256, 512, 512, 256
EARLY_BOARDS = 2
PARTS = 2
PART = SLOTS // PARTS
PART_BYTES = 2 * PACK * PART

FLOPS = 2 * (2 * K * HIDDEN * SLOTS) + 2 * HIDDEN * FEATURES * SLOTS


def tile_list_relayed_kernel(tc, xt_words, xt_scales, w_words, w_scales, w2_words, w2_scales, sa, sb,
                                 wb_words, wb_scales, offs, offs2, offs3, offs4, offs5, offs6, out):
    nc = tc.nc
    with ExitStack() as ctx:
        pool = ctx.enter_context(tc.tile_pool(name="held", bufs=1))
        tail = ctx.enter_context(tc.tile_pool(name="tail", bufs=1))
        psum = ctx.enter_context(tc.psum_pool(name="psum", bufs=1))

        def load_list(name, source):
            tile = pool.tile([P, SLOTS // LIST_ROWS], U16, name=name)
            nc.sync.dma_start(tile[:], source)
            return tile

        def cleared_plane(name, width, tag):
            plane = pool.tile([P, width], U8, name=name, tag=tag, align_bytes=MX_ALIGN)
            nc.vector.memset(plane[:].bitcast(I32), 0)
            return plane

        def load_scale_rows(queue, plane, scales):
            rows = scales[0].bitcast(I32)
            for u in range(LIVE_ROWS):
                queue.dma_start(plane[u:P:QUADRANT, :].bitcast(I32), rows[u : QUADRANTS * LIVE_ROWS : LIVE_ROWS, :])

        def load_words(name, words, tag):
            tile = pool.tile([P, HIDDEN], U32, name=name, tag=tag, align_bytes=MX_ALIGN)
            nc.sync.dma_start(tile[:].bitcast(I32), words[0].rearrange("p c i -> p (c i)").bitcast(I32))
            return tile

        def load_row_weights(name, weights):
            tile = pool.tile([P, PACK], F32, name=name)
            nc.sync.dma_start(tile[:], weights.rearrange("(p i) o -> p (i o)", i=PACK))
            return tile

        def cleared_board(engine, name, i):
            board = pool.tile([P, BOARD], F32, name="%s%d" % (name, i), tag="board%d" % i, align_bytes=MX_ALIGN)
            engine.memset(board[:], 0.0)
            return board

        def gather_tokens(name, offsets, codes_tag):
            codes = pool.tile([P, SLOTS], U16, name=name + "_codes", tag=codes_tag, align_bytes=MX_ALIGN)
            nc.vector.tensor_copy(codes[:], xt_table[:].indirect(offsets[:]))
            scales = pool.tile([P, SLOTS], U8, name=name + "_scales", tag="token_scales", align_bytes=MX_ALIGN)
            nc.vector.tensor_copy(scales[:], xt_plane[:].indirect(offsets[:]))
            return codes, scales

        xt_plane = cleared_plane("xt_plane", TOKENS, "xt_plane")
        list1 = load_list("list1", offs)
        w_staged = pool.tile([LIVE_ROWS, QUADRANTS, HIDDEN // 4], I32, name="w_staged")
        nc.sync.dma_start(w_staged[:], w_scales[0].bitcast(I32).rearrange("(q u) c -> u q c", u=LIVE_ROWS))
        load_scale_rows(nc.scalar, xt_plane, xt_scales)
        xt_table = pool.tile([P, TOKENS], U16, name="xt_table")
        nc.sync.dma_start(xt_table[:].bitcast(I32), xt_words[0].bitcast(I32))
        w_raw = load_words("w_raw", w_words, "board2")
        list3 = load_list("list3", offs3)
        sa_cols = load_row_weights("sa_cols", sa)
        w2_raw = load_words("w2_raw", w2_words, "w2_raw")
        list2 = load_list("list2", offs2)

        w_plane = cleared_plane("w_plane", HIDDEN, "board3")
        w2_plane = cleared_plane("w2_plane", HIDDEN, "w2_plane")
        load_scale_rows(nc.sync, w2_plane, w2_scales)
        boards_a = [cleared_board(nc.vector, "board_a", i) for i in range(EARLY_BOARDS)]
        list4 = load_list("list4", offs4)
        sb_cols = load_row_weights("sb_cols", sb)
        list5 = load_list("list5", offs5)
        list6 = load_list("list6", offs6)
        wb_codes = pool.tile([P, E2M1_BYTES * FEATURES], U8, name="wb_codes", align_bytes=MX_ALIGN)
        nc.sync.dma_start(wb_codes[:].bitcast(I32), wb_words[0].bitcast(I32))
        wb_plane = cleared_plane("wb_plane", FEATURES, "wb_plane")
        load_scale_rows(nc.sync, wb_plane, wb_scales)

        for q in range(QUADRANTS):
            nc.vector.tensor_copy(w_plane[QUADRANT * q : QUADRANT * q + LIVE_ROWS, :].bitcast(I32), w_staged[:, q, :])
        w_plane_by_slice = w_plane[:].rearrange("p (m i) -> p i m", i=PACK)
        w_raw_by_column = w_raw[:].rearrange("p (m i) -> p m i", i=PACK)
        first_scales = pool.tile([P, P], U8, name="first_scales", tag="dealt_scales", align_bytes=MX_ALIGN)
        nc.vector.tensor_copy(first_scales[:], w_plane_by_slice[:, 0, :])
        x1_codes, x1_scales = gather_tokens("x1", list1, "x1_codes")
        first_codes = pool.tile([P, P], U32, name="first_codes", tag="first_codes", align_bytes=MX_ALIGN)
        nc.scalar.copy(first_codes[:], w_raw_by_column[:, :, 0])
        later_codes = pool.tile([P, PACK - 1, P], U32, name="later_codes", tag="dealt_codes", align_bytes=MX_ALIGN)
        nc.scalar.copy(later_codes[:].rearrange("p i m -> p m i"), w_raw_by_column[:, :, 1:PACK])
        w_codes = [first_codes[:]] + [later_codes[:, i, :] for i in range(PACK - 1)]
        w_dealt_scales = [first_scales[:]]

        for i in range(PACK):
            a_sum = psum.tile([P, SLOTS], F32, name="a_sum%d" % i, tag="bank%d" % i)
            nc.tensor.matmul_mx(a_sum[:], lhsT=w_codes[i].bitcast(E4M3), lhsT_scale=w_dealt_scales[i],
                                rhs=x1_codes[:].bitcast(E2M1), rhs_scale=x1_scales[:], start=True, stop=True)
            a_rows = pool.tile([P, SLOTS], F32, name="a_rows%d" % i)
            if i == 0:
                nc.scalar.copy(a_rows[:], a_sum[:])
                later_scales = pool.tile([P, PACK - 1, P], U8, name="later_scales", tag="dealt_scales", align_bytes=MX_ALIGN)
                nc.vector.tensor_copy(later_scales[:], w_plane_by_slice[:, 1:PACK, :])
                w_dealt_scales.extend(later_scales[:, later, :] for later in range(PACK - 1))
            else:
                nc.vector.tensor_copy(a_rows[:], a_sum[:])
            if i >= EARLY_BOARDS:
                boards_a.append(cleared_board(nc.gpsimd, "board_a", i))
            nc.scalar.activation(boards_a[i][:].indirect(list3[:]), a_rows[:], COPY, scale=sa_cols[:, i : i + 1])

        x2_codes, x2_scales = gather_tokens("x2", list2, "first_codes")
        w2_codes = pool.tile([P, PACK, P], U32, name="w2_codes", tag="dealt_codes", align_bytes=MX_ALIGN)
        nc.vector.tensor_copy(w2_codes[:].rearrange("p i m -> p m i"), w2_raw[:].rearrange("p (m i) -> p m i", i=PACK))
        w2_dealt_scales = pool.tile([P, PACK, P], U8, name="w2_dealt_scales", tag="dealt_scales", align_bytes=MX_ALIGN)
        nc.vector.tensor_copy(w2_dealt_scales[:], w2_plane[:].rearrange("p (m i) -> p i m", i=PACK))

        boards_b = []
        for i in range(PACK):
            b_sum = psum.tile([P, SLOTS], F32, name="b_sum%d" % i)
            nc.tensor.matmul_mx(b_sum[:], lhsT=w2_codes[:, i, :].bitcast(E5M2), lhsT_scale=w2_dealt_scales[:, i, :],
                                rhs=x2_codes[:].bitcast(E2M1), rhs_scale=x2_scales[:], start=True, stop=True)
            picked = pool.tile([P, SLOTS], F32, name="picked%d" % i, tag=("w2_raw", "w2_plane")[i % 2], align_bytes=MX_ALIGN)
            nc.vector.tensor_copy(picked[:], boards_a[i][:].indirect(list4[:]))
            if i == PACK - 1:
                diff = tail.tile([P, SLOTS], F32, name="diff%d" % i, offset=PART_BYTES // 2, align_bytes=MX_ALIGN)
            else:
                diff = pool.tile([P, SLOTS], F32, name="diff%d" % i)
            nc.vector.tensor_tensor(diff[:], picked[:], b_sum[:], ALU.subtract)
            h1 = pool.tile([P, SLOTS], F32, name="h1_%d" % i)
            nc.vector.scalar_tensor_tensor(h1[:], diff[:], -1.0, diff[:], ALU.mult, ALU.max)
            boards_b.append(cleared_board(nc.gpsimd, "board_b", i))
            nc.scalar.activation(boards_b[i][:].indirect(list5[:]), h1[:], COPY, scale=sb_cols[:, i : i + 1])

        out_rows = out.rearrange("(h p) o -> h p o", p=P)
        for part in range(PARTS):
            places = slice(part * PART, (part + 1) * PART)
            hid = tail.tile([P, PACK * PART], BF16, name="hid%d" % part, offset=PART_BYTES * part, align_bytes=MX_ALIGN)
            offsets = list6[:, part * PART // LIST_ROWS : (part + 1) * PART // LIST_ROWS]
            for i in range(PACK):
                nc.scalar.activation(hid[:, i : PACK * PART : PACK], boards_b[i][:].indirect(offsets), COPY)
            hid_codes = pool.tile([P, PART], U32, name="hid_codes%d" % part, align_bytes=MX_ALIGN)
            hid_scales = pool.tile([P, PART], U8, name="hid_scales%d" % part, align_bytes=MX_ALIGN)
            nc.vector.quantize_mx(hid_codes[:].bitcast(E5M2), hid_scales[:], hid[:])
            for h in range(FEATURES // P):
                out_sum = psum.tile([P, PART], F32, name="out_sum%d%d" % (part, h), tag="bank%d" % (FEATURES // P * part + h))
                nc.tensor.matmul_mx(out_sum[:], lhsT=wb_codes[:, E2M1_BYTES * P * h : E2M1_BYTES * P * (h + 1)].bitcast(E2M1),
                                    lhsT_scale=wb_plane[:, P * h : P * (h + 1)],
                                    rhs=hid_codes[:].bitcast(E5M2), rhs_scale=hid_scales[:], start=True, stop=True)
                result = pool.tile([P, PART], F32, name="result%d%d" % (part, h))
                if part == PARTS - 1 and h == 0:
                    nc.scalar.copy(result[:], out_sum[:])
                    nc.scalar.dma_start(out_rows[h, :, places], result[:])
                else:
                    nc.vector.tensor_copy(result[:], out_sum[:])
                    nc.sync.dma_start(out_rows[h, :, places], result[:])
